import numpy as np, ml_dtypes
CORES = [71,199,95,223,103,231,111,239,119,247,127,255]
N = 12
import mx_ref
NC, KT = 256, 1
FROM = [11,4,0,9,6,7,8,10,2,1,5,3]
BF = ml_dtypes.bfloat16
def setup_inputs(rng):
    def f(*shape):
        return mx_ref.flush((rng.standard_normal(shape, dtype=np.float32) * np.exp2(rng.integers(-2, 3, shape[:-1] + (1,)))).astype(BF))
    return {"w": f(N, 128, KT * 512), "x": f(N, 128, KT * 4 * NC)}
def setup_inputs_blocks(rng):
    d = setup_inputs(rng)
    for k in ("w", "x"): d[k] = mx_ref.spread(d[k], rng, 4)
    return d
def setup_inputs_wide(rng):
    d = setup_inputs(rng)
    for k in ("w", "x"): d[k] = mx_ref.flush((d[k].astype(np.float32) * np.exp2(rng.integers(-8, 9, (N, 1, 1))).astype(np.float32)).astype(BF))
    return d
def setup_inputs_zeros(rng):
    d = setup_inputs(rng); v = d["x"].reshape(N, 128, -1, 4).copy()
    v[np.broadcast_to((rng.random((N, 1, v.shape[2], 1)) < 0.33), v.shape)] = 0
    d["x"] = v.reshape(d["x"].shape)
    return d
def reference(w, x):
    y = np.zeros((N, 128, NC), np.float32)
    for r in range(N):
        for t in range(KT):
            p = mx_ref.matmul(mx_ref.quantize(w[r][:, 512 * t:512 * t + 512]), mx_ref.quantize(x[FROM[r]][:, 4 * NC * t:4 * NC * t + 4 * NC]))
            y[r] = p if t == 0 else y[r] + p
    return {"y": y}

@@ -1,0 +1,63 @@
+from concourse.mybir import dt, ActivationFunctionType
+
+NC = 256
+MC = 128
+HALF = NC // 2
+
+SCRATCH = {
+    "xs": ("sbuf", [128, 4 * NC], "bfloat16"),
+    "ws": ("sbuf", [128, 4 * MC], "bfloat16"),
+    "xq": ("sbuf", [128, NC], "float8_e4m3fn_x4"),
+    "xp": ("sbuf", [128, NC], "uint8"),
+    "wq": ("sbuf", [128, MC], "float8_e4m3fn_x4"),
+    "wp": ("sbuf", [128, MC], "uint8"),
+    "lq": ("sbuf", [128, NC], "float8_e4m3fn_x4"),
+    "lp": ("sbuf", [128, NC], "uint8"),
+    "acc": ("psum", [128, 1024], "float32"),
+    "yb": ("sbuf", [128, NC], "float32"),
+}
+SEMAPHORES = ["xin", "win", "xpacked", "wpacked", "sent", "arrived", "mm0", "mm1", "copied", "stored"]
+
+
+def rank_program(g, core, T, topo):
+    rank = T.rank_of(core)
+    if rank is None:
+        return
+    S = T.sem
+    dst = T.cores[T.tables["FROM"].index(rank)]
+
+    g.sync.dma_start(T.xs[:], T.x[:]).then_inc(S.xin, 16)
+    g.sync.dma_start(T.ws[:], T.w[:]).then_inc(S.win, 16)
+
+    g.vector.wait_ge(S.xin, 16)
+    g.vector.quantize_mx(T.xq[:], T.xp[:], T.xs[:]).then_inc(S.xpacked, 1)
+    g.vector.wait_ge(S.win, 16)
+    g.vector.quantize_mx(T.wq[:], T.wp[:], T.ws[:]).then_inc(S.wpacked, 1)
+
+    rid, pid = topo.addr(dst, core)
+    mask = topo.mask(core, dst)
+    engines = bin(mask).count("1")
+    g.wait_ge(S.xpacked, 1)
+    g.remote_dma(out_ap=T.lq[:].bitcast(dt.uint8), in_ap=T.xq[:].bitcast(dt.uint8), remote_sem=S.arrived,
+                 local_sem=S.sent, pid=pid, routing_id=rid, dma_engine_mask=mask)
+    g.remote_dma(out_ap=T.lp[:], in_ap=T.xp[:], remote_sem=S.arrived,
+                 local_sem=S.sent, pid=pid, routing_id=rid, dma_engine_mask=mask)
+
+    src = T.cores[T.tables["FROM"][rank]]
+    landed = 2 * bin(topo.mask(src, core)).count("1")
+    g.tensor.wait_ge(S.wpacked, 1)
+    g.tensor.wait_ge(S.arrived, landed)
+    g.tensor.matmul_mx(T.acc[:, 0:HALF], T.wq[:], T.wp[:], T.lq[:, 0:HALF], T.lp[:, 0:HALF],
+                       True, True).then_inc(S.mm0, 1)
+    g.tensor.matmul_mx(T.acc[:, 512:512 + HALF], T.wq[:], T.wp[:], T.lq[:, HALF:NC], T.lp[:, HALF:NC],
+                       True, True).then_inc(S.mm1, 1)
+
+    g.vector.wait_ge(S.mm0, 1)
+    g.vector.tensor_copy(T.yb[:, 0:HALF], T.acc[:, 0:HALF]).then_inc(S.copied, 1)
+    g.scalar.wait_ge(S.mm1, 1)
+    g.scalar.activation(T.yb[:, HALF:NC], T.acc[:, 512:512 + HALF], ActivationFunctionType.Copy).then_inc(S.copied, 1)
+
+    g.sync.wait_ge(S.copied, 2)
+    g.sync.dma_start(T.y[:], T.yb[:]).then_inc(S.stored, 16)
+    g.sync.wait_ge(S.stored, 16)
+    g.wait_ge(S.sent, 2 * engines)

@@ -2,7 +2,7 @@ from concourse.mybir import dt, ActivationFunctionType
 
 NC = 256
 MC = 128
-HALF = NC // 2
+H = NC // 2
 
 SCRATCH = {
     "xs": ("sbuf", [128, 4 * NC], "bfloat16"),
@@ -16,7 +16,8 @@ SCRATCH = {
     "acc": ("psum", [128, 1024], "float32"),
     "yb": ("sbuf", [128, NC], "float32"),
 }
-SEMAPHORES = ["xin", "win", "xpacked", "wpacked", "sent", "arrived", "mm0", "mm1", "copied", "stored"]
+SEMAPHORES = ["xin0", "xin1", "win", "xpk0", "xpk1", "wpk", "sent", "arr0", "arr1", "mm0", "mm1",
+              "cp0", "cp1", "stored"]
 
 
 def rank_program(g, core, T, topo):
@@ -25,39 +26,48 @@ def rank_program(g, core, T, topo):
         return
     S = T.sem
     dst = T.cores[T.tables["FROM"].index(rank)]
+    src = T.cores[T.tables["FROM"][rank]]
+    half = [slice(H * h, H * (h + 1)) for h in range(2)]
+    half4 = [slice(4 * H * h, 4 * H * (h + 1)) for h in range(2)]
 
-    g.sync.dma_start(T.xs[:], T.x[:]).then_inc(S.xin, 16)
+    for h in range(2):
+        g.sync.dma_start(T.xs[:, half4[h]], T.x[:, half4[h]]).then_inc(S["xin%d" % h], 16)
     g.sync.dma_start(T.ws[:], T.w[:]).then_inc(S.win, 16)
 
-    g.vector.wait_ge(S.xin, 16)
-    g.vector.quantize_mx(T.xq[:], T.xp[:], T.xs[:]).then_inc(S.xpacked, 1)
+    for h in range(2):
+        g.vector.wait_ge(S["xin%d" % h], 16)
+        g.vector.quantize_mx(T.xq[:, half[h]], T.xp[:, half[h]], T.xs[:, half4[h]]).then_inc(S["xpk%d" % h], 1)
     g.vector.wait_ge(S.win, 16)
-    g.vector.quantize_mx(T.wq[:], T.wp[:], T.ws[:]).then_inc(S.wpacked, 1)
+    g.vector.quantize_mx(T.wq[:], T.wp[:], T.ws[:]).then_inc(S.wpk, 1)
 
     rid, pid = topo.addr(dst, core)
     mask = topo.mask(core, dst)
     engines = bin(mask).count("1")
-    g.wait_ge(S.xpacked, 1)
-    g.remote_dma(out_ap=T.lq[:].bitcast(dt.uint8), in_ap=T.xq[:].bitcast(dt.uint8), remote_sem=S.arrived,
-                 local_sem=S.sent, pid=pid, routing_id=rid, dma_engine_mask=mask)
-    g.remote_dma(out_ap=T.lp[:], in_ap=T.xp[:], remote_sem=S.arrived,
-                 local_sem=S.sent, pid=pid, routing_id=rid, dma_engine_mask=mask)
 
-    src = T.cores[T.tables["FROM"][rank]]
-    landed = 2 * bin(topo.mask(src, core)).count("1")
-    g.tensor.wait_ge(S.wpacked, 1)
-    g.tensor.wait_ge(S.arrived, landed)
-    g.tensor.matmul_mx(T.acc[:, 0:HALF], T.wq[:], T.wp[:], T.lq[:, 0:HALF], T.lp[:, 0:HALF],
-                       True, True).then_inc(S.mm0, 1)
-    g.tensor.matmul_mx(T.acc[:, 512:512 + HALF], T.wq[:], T.wp[:], T.lq[:, HALF:NC], T.lp[:, HALF:NC],
-                       True, True).then_inc(S.mm1, 1)
+    def send(out_ap, in_ap, sem):
+        g.remote_dma(out_ap=out_ap, in_ap=in_ap, remote_sem=sem, local_sem=S.sent,
+                     pid=pid, routing_id=rid, dma_engine_mask=mask)
+
+    g.wait_ge(S.xpk0, 1)
+    send(T.lq[:, half[0]].bitcast(dt.uint8), T.xq[:, half[0]].bitcast(dt.uint8), S.arr0)
+    g.wait_ge(S.xpk1, 1)
+    send(T.lp[:], T.xp[:], S.arr0)
+    send(T.lq[:, half[1]].bitcast(dt.uint8), T.xq[:, half[1]].bitcast(dt.uint8), S.arr1)
+
+    per_write = bin(topo.mask(src, core)).count("1")
+    g.tensor.wait_ge(S.wpk, 1)
+    for h in range(2):
+        g.tensor.wait_ge(S["arr%d" % h], (2 - h) * per_write)
+        g.tensor.matmul_mx(T.acc[:, 512 * h:512 * h + H], T.wq[:], T.wp[:], T.lq[:, half[h]], T.lp[:, half[h]],
+                           True, True).then_inc(S["mm%d" % h], 1)
 
     g.vector.wait_ge(S.mm0, 1)
-    g.vector.tensor_copy(T.yb[:, 0:HALF], T.acc[:, 0:HALF]).then_inc(S.copied, 1)
+    g.vector.tensor_copy(T.yb[:, half[0]], T.acc[:, 0:H]).then_inc(S.cp0, 1)
     g.scalar.wait_ge(S.mm1, 1)
-    g.scalar.activation(T.yb[:, HALF:NC], T.acc[:, 512:512 + HALF], ActivationFunctionType.Copy).then_inc(S.copied, 1)
+    g.scalar.activation(T.yb[:, half[1]], T.acc[:, 512:512 + H], ActivationFunctionType.Copy).then_inc(S.cp1, 1)
 
-    g.sync.wait_ge(S.copied, 2)
-    g.sync.dma_start(T.y[:], T.yb[:]).then_inc(S.stored, 16)
-    g.sync.wait_ge(S.stored, 16)
-    g.wait_ge(S.sent, 2 * engines)
+    for h in range(2):
+        g.sync.wait_ge(S["cp%d" % h], 1)
+        g.sync.dma_start(T.y[:, half[h]], T.yb[:, half[h]]).then_inc(S.stored, 16)
+    g.sync.wait_ge(S.stored, 32)
+    g.wait_ge(S.sent, 3 * engines)

from concourse.mybir import dt, ActivationFunctionType

NC = 256
MC = 128
H = NC // 2

SCRATCH = {
    "xs": ("sbuf", [128, 4 * NC], "bfloat16"),
    "ws": ("sbuf", [128, 4 * MC], "bfloat16"),
    "xq": ("sbuf", [128, NC], "float8_e4m3fn_x4"),
    "xp": ("sbuf", [128, NC], "uint8"),
    "wq": ("sbuf", [128, MC], "float8_e4m3fn_x4"),
    "wp": ("sbuf", [128, MC], "uint8"),
    "lq": ("sbuf", [128, NC], "float8_e4m3fn_x4"),
    "lp": ("sbuf", [128, NC], "uint8"),
    "acc": ("psum", [128, 1024], "float32"),
    "yb": ("sbuf", [128, NC], "float32"),
}
SEMAPHORES = ["xin0", "xin1", "win", "xpk0", "xpk1", "wpk", "sent", "arr0", "arr1", "mm0", "mm1",
              "cp0", "cp1", "stored"]


def rank_program(g, core, T, topo):
    rank = T.rank_of(core)
    if rank is None:
        return
    S = T.sem
    dst = T.cores[T.tables["FROM"].index(rank)]
    src = T.cores[T.tables["FROM"][rank]]
    half = [slice(H * h, H * (h + 1)) for h in range(2)]
    half4 = [slice(4 * H * h, 4 * H * (h + 1)) for h in range(2)]

    for h in range(2):
        g.sync.dma_start(T.xs[:, half4[h]], T.x[:, half4[h]]).then_inc(S["xin%d" % h], 16)
    g.sync.dma_start(T.ws[:], T.w[:]).then_inc(S.win, 16)

    for h in range(2):
        g.vector.wait_ge(S["xin%d" % h], 16)
        g.vector.quantize_mx(T.xq[:, half[h]], T.xp[:, half[h]], T.xs[:, half4[h]]).then_inc(S["xpk%d" % h], 1)
    g.vector.wait_ge(S.win, 16)
    g.vector.quantize_mx(T.wq[:], T.wp[:], T.ws[:]).then_inc(S.wpk, 1)

    rid, pid = topo.addr(dst, core)
    mask = topo.mask(core, dst)
    engines = bin(mask).count("1")

    def send(out_ap, in_ap, sem):
        g.remote_dma(out_ap=out_ap, in_ap=in_ap, remote_sem=sem, local_sem=S.sent,
                     pid=pid, routing_id=rid, dma_engine_mask=mask)

    g.wait_ge(S.xpk0, 1)
    send(T.lq[:, half[0]].bitcast(dt.uint8), T.xq[:, half[0]].bitcast(dt.uint8), S.arr0)
    g.wait_ge(S.xpk1, 1)
    send(T.lp[:], T.xp[:], S.arr0)
    send(T.lq[:, half[1]].bitcast(dt.uint8), T.xq[:, half[1]].bitcast(dt.uint8), S.arr1)

    per_write = bin(topo.mask(src, core)).count("1")
    g.tensor.wait_ge(S.wpk, 1)
    for h in range(2):
        g.tensor.wait_ge(S["arr%d" % h], (2 - h) * per_write)
        g.tensor.matmul_mx(T.acc[:, 512 * h:512 * h + H], T.wq[:], T.wp[:], T.lq[:, half[h]], T.lp[:, half[h]],
                           True, True).then_inc(S["mm%d" % h], 1)

    g.vector.wait_ge(S.mm0, 1)
    g.vector.tensor_copy(T.yb[:, half[0]], T.acc[:, 0:H]).then_inc(S.cp0, 1)
    g.scalar.wait_ge(S.mm1, 1)
    g.scalar.activation(T.yb[:, half[1]], T.acc[:, 512:512 + H], ActivationFunctionType.Copy).then_inc(S.cp1, 1)

    for h in range(2):
        g.sync.wait_ge(S["cp%d" % h], 1)
        g.sync.dma_start(T.y[:, half[h]], T.yb[:, half[h]]).then_inc(S.stored, 16)
    g.sync.wait_ge(S.stored, 32)
    g.wait_ge(S.sent, 3 * engines)
